import numpy as np
import ml_dtypes


def mxq(x, axis, fmt="e4m3"):
    dtype, down = {"e4m3": (ml_dtypes.float8_e4m3fn, 7), "e5m2": (ml_dtypes.float8_e5m2, 14)}[fmt]
    v = np.moveaxis(np.asarray(x, np.float32).astype(ml_dtypes.bfloat16).astype(np.float64), axis, -1)
    blocks = v.reshape(v.shape[:-1] + (-1, 32))
    amax = np.abs(blocks).max(-1, keepdims=True)
    byte = np.maximum(np.where(amax > 0, np.frexp(amax)[1] - 1 + 127, 0) - down, 1)
    scale = np.exp2(byte - 127.0)
    codes = (blocks / scale).astype(np.float32).astype(dtype).astype(np.float64)
    return np.moveaxis((codes * scale).reshape(v.shape), -1, axis)


WIDE = False


def mx_kscale(k):
    if not WIDE:
        return np.ones(k)
    levels = np.array([10, -10, 5, -5, 0])
    if k % 512:
        return np.exp2(np.random.permutation(np.resize(levels, k // 32))).repeat(32)
    a = np.empty((k // 512, 16))
    for p in range(k // 512):
        a[p, :8] = np.random.permutation(np.resize(levels, 8))
        for g in range(8):
            far = levels[np.abs(levels - a[p, g]) >= 10]
            a[p, g + 8] = far[np.random.randint(len(far))]
    return np.exp2(a.ravel()).repeat(32)


def f64(x):
    return np.asarray(x).astype(np.float64)


def striped(idx):
    return np.tile(idx.reshape(-1, 16).T, (8, 1)).astype(np.uint16)


def unstriped(offs):
    return offs[:16].T.reshape(-1).astype(np.int64)


K, T, E, C, N = 512, 2048, 8, 256, 256


def by_expert(wq, xq):
    return np.concatenate([wq[e].T @ xq[:, e * C:(e + 1) * C] for e in range(E)], axis=1)


def setup_inputs():
    n = np.random.standard_normal
    s = mx_kscale(K)[:, None]
    return {
        "xT": (n((K, T)) * s).astype(np.float32),
        "w": (n((E, K, N)) / np.sqrt(K) / s[None]).astype(np.float32),
        "gate": np.tile(np.random.uniform(0.2, 1.0, E * C), (N, 1)).astype(np.float32),
        "offs": striped(np.random.permutation(T)[:E * C]),
    }


def reference(xT, w, gate, offs):
    idx = unstriped(offs)
    xq = mxq(f64(xT)[:, idx], 0, "e4m3")
    y = by_expert(mxq(f64(w), 1, "e4m3"), xq)
    out = np.zeros((N, T))
    out[:, idx] = f64(gate) * y
    return out

@@ -1,0 +1,145 @@
+from contextlib import ExitStack
+
+import concourse.mybir as mybir
+
+K, T, E, C, N = 512, 2048, 8, 256, 256
+FLOPS = 2 * K * N * E * C
+
+F32 = mybir.dt.float32
+BF16 = mybir.dt.bfloat16
+U32 = mybir.dt.uint32
+U16 = mybir.dt.uint16
+U8 = mybir.dt.uint8
+FP8X4 = mybir.dt.float8_e4m3fn_x4
+MULT = mybir.AluOpType.mult
+
+P = 128
+PACK = 4
+SLICE = 512
+N_SLICES = E * C // SLICE
+EXPERTS_A_SLICE = SLICE // C
+BLOCKS = N // P
+
+
+def tile_routed_moe_kernel(tc, xT, w, gate, offs, out):
+    nc = tc.nc
+    with ExitStack() as ctx:
+        lists = ctx.enter_context(tc.tile_pool(name="lists", bufs=1))
+        keep = ctx.enter_context(tc.tile_pool(name="keep", bufs=1))
+        psum = ctx.enter_context(tc.psum_pool(name="psum", bufs=1))
+
+        offsets = lists.tile([P, E * C // 16], U16, name="offsets")
+        nc.sync.dma_start(offsets[:], offs)
+
+        def slice_offsets(s):
+            return offsets[:, s * (SLICE // 16) : (s + 1) * (SLICE // 16)]
+
+        x_rows = xT.rearrange("(p t) n -> p t n", t=PACK)
+        planes = [keep.tile([P, T], F32, name="plane%d" % t) for t in range(PACK)]
+        w_raw = [keep.tile([P, PACK, N], F32, name="w_raw%d" % e) for e in range(E)]
+        gates = [keep.tile([P, E * C], F32, name="gate%d" % b) for b in range(BLOCKS)]
+
+        def load_plane(t):
+            nc.sync.dma_start(planes[t][:], x_rows[:, t, :])
+
+        def load_w(e):
+            nc.sync.dma_start(w_raw[e][:], w[e].rearrange("(p j) n -> p j n", j=PACK))
+
+        load_plane(0)
+        load_w(0)
+        load_w(1)
+        load_plane(1)
+        load_w(2)
+        load_w(3)
+        load_plane(2)
+        load_w(4)
+        load_w(5)
+        load_w(6)
+        load_w(7)
+        load_plane(3)
+        for b in range(BLOCKS):
+            nc.sync.dma_start(gates[b][:], gate[b * P : (b + 1) * P, :])
+
+        w_codes = keep.tile([P, E * N], U32, name="w_codes", align_bytes=64)
+        w_scales = keep.tile([P, E * N], U8, name="w_scales", align_bytes=64)
+        x_codes = keep.tile([P, E * C], U32, name="x_codes", align_bytes=64)
+        x_scales = keep.tile([P, E * C], U8, name="x_scales", align_bytes=64)
+        windows = [keep.tile([P, T], F32, name="window%d" % b) for b in range(BLOCKS)]
+        sums = [
+            [keep.tile([P, SLICE], F32, name="sums%d_%d" % (b, s)) for s in range(N_SLICES)]
+            for b in range(BLOCKS)
+        ]
+        gathered = [keep.tile([P, PACK, SLICE], F32, name="gathered%d" % s) for s in range(N_SLICES)]
+
+        def gather_plane(t):
+            for s in range(N_SLICES):
+                nc.vector.tensor_copy(gathered[s][:, t, :], planes[t][:].indirect(slice_offsets(s)))
+
+        def weights(s):
+            w_grouped = keep.tile([P, EXPERTS_A_SLICE, N, PACK], BF16, name="w_grouped%d" % s, align_bytes=64)
+            for i in range(EXPERTS_A_SLICE):
+                nc.scalar.copy(w_grouped[:, i, :, :], w_raw[s * EXPERTS_A_SLICE + i][:].rearrange("p j n -> p n j"))
+            cols = slice(s * SLICE, (s + 1) * SLICE)
+            nc.vector.quantize_mx(
+                out=w_codes[:, cols].bitcast(FP8X4),
+                scales=w_scales[:, cols],
+                in_=w_grouped[:].rearrange("p i n j -> p (i n j)"),
+            )
+
+        def tokens(s):
+            x_grouped = keep.tile([P, SLICE, PACK], BF16, name="x_grouped%d" % s, align_bytes=64)
+            nc.scalar.copy(x_grouped[:], gathered[s][:].rearrange("p t n -> p n t"))
+            cols = slice(s * SLICE, (s + 1) * SLICE)
+            nc.vector.quantize_mx(
+                out=x_codes[:, cols].bitcast(FP8X4),
+                scales=x_scales[:, cols],
+                in_=x_grouped[:].rearrange("p n t -> p (n t)"),
+            )
+
+        def multiply(s):
+            for b in range(BLOCKS):
+                acc = psum.tile([P, SLICE], F32, name="acc%d_%d" % (b, s))
+                for i in range(EXPERTS_A_SLICE):
+                    e = s * EXPERTS_A_SLICE + i
+                    feats = slice(e * N + b * P, e * N + (b + 1) * P)
+                    slots = slice(e * C, (e + 1) * C)
+                    nc.tensor.matmul_mx(
+                        out=acc[:, i * C : (i + 1) * C],
+                        lhsT=w_codes[:, feats].bitcast(FP8X4),
+                        lhsT_scale=w_scales[:, feats],
+                        rhs=x_codes[:, slots].bitcast(FP8X4),
+                        rhs_scale=x_scales[:, slots],
+                        start=True,
+                        stop=True,
+                    )
+                nc.scalar.copy(sums[b][s][:], acc[:])
+
+        def scatter(b, s):
+            nc.vector.tensor_tensor(
+                windows[b][:].indirect(slice_offsets(s)),
+                sums[b][s][:],
+                gates[b][:, s * SLICE : (s + 1) * SLICE],
+                MULT,
+            )
+
+        gather_plane(0)
+        weights(0)
+        gather_plane(1)
+        weights(1)
+        gather_plane(2)
+        weights(2)
+        weights(3)
+        gather_plane(3)
+        tokens(0)
+        tokens(1)
+        multiply(0)
+        tokens(2)
+        multiply(1)
+        tokens(3)
+        multiply(2)
+        multiply(3)
+        for s in range(N_SLICES):
+            for b in range(BLOCKS):
+                scatter(b, s)
+        for b in range(BLOCKS):
+            nc.sync.dma_start(out[b * P : (b + 1) * P, :], windows[b][:])

@@ -35,12 +35,12 @@ def tile_routed_moe_kernel(tc, xT, w, gate, offs, out):
             return offsets[:, s * (SLICE // 16) : (s + 1) * (SLICE // 16)]
 
         x_rows = xT.rearrange("(p t) n -> p t n", t=PACK)
-        planes = [keep.tile([P, T], F32, name="plane%d" % t) for t in range(PACK)]
+        planes = keep.tile([P, PACK, T], F32, name="planes")
         w_raw = [keep.tile([P, PACK, N], F32, name="w_raw%d" % e) for e in range(E)]
         gates = [keep.tile([P, E * C], F32, name="gate%d" % b) for b in range(BLOCKS)]
 
         def load_plane(t):
-            nc.sync.dma_start(planes[t][:], x_rows[:, t, :])
+            nc.sync.dma_start(planes[:, t, :], x_rows[:, t, :])
 
         def load_w(e):
             nc.sync.dma_start(w_raw[e][:], w[e].rearrange("(p j) n -> p j n", j=PACK))
@@ -69,11 +69,12 @@ def tile_routed_moe_kernel(tc, xT, w, gate, offs, out):
             [keep.tile([P, SLICE], F32, name="sums%d_%d" % (b, s)) for s in range(N_SLICES)]
             for b in range(BLOCKS)
         ]
-        gathered = [keep.tile([P, PACK, SLICE], F32, name="gathered%d" % s) for s in range(N_SLICES)]
+        x_grouped = [
+            keep.tile([P, SLICE, PACK], BF16, name="x_grouped%d" % s, align_bytes=64) for s in range(N_SLICES)
+        ]
 
-        def gather_plane(t):
-            for s in range(N_SLICES):
-                nc.vector.tensor_copy(gathered[s][:, t, :], planes[t][:].indirect(slice_offsets(s)))
+        def gather(s, t):
+            nc.vector.tensor_copy(x_grouped[s][:, :, t], planes[:, t, :].indirect(slice_offsets(s)))
 
         def weights(s):
             w_grouped = keep.tile([P, EXPERTS_A_SLICE, N, PACK], BF16, name="w_grouped%d" % s, align_bytes=64)
@@ -86,14 +87,12 @@ def tile_routed_moe_kernel(tc, xT, w, gate, offs, out):
                 in_=w_grouped[:].rearrange("p i n j -> p (i n j)"),
             )
 
-        def tokens(s):
-            x_grouped = keep.tile([P, SLICE, PACK], BF16, name="x_grouped%d" % s, align_bytes=64)
-            nc.scalar.copy(x_grouped[:], gathered[s][:].rearrange("p t n -> p n t"))
+        def quantize_tokens(s):
             cols = slice(s * SLICE, (s + 1) * SLICE)
             nc.vector.quantize_mx(
                 out=x_codes[:, cols].bitcast(FP8X4),
                 scales=x_scales[:, cols],
-                in_=x_grouped[:].rearrange("p n t -> p (n t)"),
+                in_=x_grouped[s][:].rearrange("p n t -> p (n t)"),
             )
 
         def multiply(s):
@@ -122,22 +121,20 @@ def tile_routed_moe_kernel(tc, xT, w, gate, offs, out):
                 MULT,
             )
 
-        gather_plane(0)
+        for s in range(N_SLICES):
+            gather(s, 0)
         weights(0)
-        gather_plane(1)
+        for s in range(N_SLICES):
+            gather(s, 1)
         weights(1)
-        gather_plane(2)
+        for s in range(N_SLICES):
+            gather(s, 2)
         weights(2)
         weights(3)
-        gather_plane(3)
-        tokens(0)
-        tokens(1)
-        multiply(0)
-        tokens(2)
-        multiply(1)
-        tokens(3)
-        multiply(2)
-        multiply(3)
+        for s in range(N_SLICES):
+            gather(s, 3)
+            quantize_tokens(s)
+            multiply(s)
         for s in range(N_SLICES):
             for b in range(BLOCKS):
                 scatter(b, s)

@@ -19,6 +19,7 @@ SLICE = 512
 N_SLICES = E * C // SLICE
 EXPERTS_A_SLICE = SLICE // C
 BLOCKS = N // P
+COPY = mybir.ActivationFunctionType.Copy
 
 
 def tile_routed_moe_kernel(tc, xT, w, gate, offs, out):
@@ -35,30 +36,23 @@ def tile_routed_moe_kernel(tc, xT, w, gate, offs, out):
             return offsets[:, s * (SLICE // 16) : (s + 1) * (SLICE // 16)]
 
         x_rows = xT.rearrange("(p t) n -> p t n", t=PACK)
-        planes = keep.tile([P, PACK, T], F32, name="planes")
+        planes = [keep.tile([P, T], F32, name="plane%d" % t) for t in range(PACK)]
+        planes_bf = keep.tile([P, PACK, T], BF16, name="planes_bf")
         w_raw = [keep.tile([P, PACK, N], F32, name="w_raw%d" % e) for e in range(E)]
         gates = [keep.tile([P, E * C], F32, name="gate%d" % b) for b in range(BLOCKS)]
 
-        def load_plane(t):
-            nc.sync.dma_start(planes[:, t, :], x_rows[:, t, :])
+        for t in range(PACK):
+            nc.sync.dma_start(planes[t][:], x_rows[:, t, :])
 
         def load_w(e):
             nc.sync.dma_start(w_raw[e][:], w[e].rearrange("(p j) n -> p j n", j=PACK))
 
-        load_plane(0)
-        load_w(0)
-        load_w(1)
-        load_plane(1)
-        load_w(2)
-        load_w(3)
-        load_plane(2)
-        load_w(4)
-        load_w(5)
-        load_w(6)
-        load_w(7)
-        load_plane(3)
+        for e in range(4):
+            load_w(e)
         for b in range(BLOCKS):
             nc.sync.dma_start(gates[b][:], gate[b * P : (b + 1) * P, :])
+        for e in range(4, E):
+            load_w(e)
 
         w_codes = keep.tile([P, E * N], U32, name="w_codes", align_bytes=64)
         w_scales = keep.tile([P, E * N], U8, name="w_scales", align_bytes=64)
@@ -69,22 +63,43 @@ def tile_routed_moe_kernel(tc, xT, w, gate, offs, out):
             [keep.tile([P, SLICE], F32, name="sums%d_%d" % (b, s)) for s in range(N_SLICES)]
             for b in range(BLOCKS)
         ]
+        accs = [
+            [psum.tile([P, SLICE], F32, name="acc%d_%d" % (b, s)) for s in range(N_SLICES)]
+            for b in range(BLOCKS)
+        ]
+        gathered = [keep.tile([P, PACK, SLICE], F32, name="gathered%d" % s) for s in range(2)]
         x_grouped = [
             keep.tile([P, SLICE, PACK], BF16, name="x_grouped%d" % s, align_bytes=64) for s in range(N_SLICES)
         ]
+        w_grouped = [
+            keep.tile([P, EXPERTS_A_SLICE, N, PACK], BF16, name="w_grouped%d" % s, align_bytes=64)
+            for s in range(N_SLICES)
+        ]
 
-        def gather(s, t):
-            nc.vector.tensor_copy(x_grouped[s][:, :, t], planes[:, t, :].indirect(slice_offsets(s)))
+        def gather_vector(s, t):
+            nc.vector.tensor_copy(gathered[s][:, t, :], planes[t][:].indirect(slice_offsets(s)))
 
-        def weights(s):
-            w_grouped = keep.tile([P, EXPERTS_A_SLICE, N, PACK], BF16, name="w_grouped%d" % s, align_bytes=64)
+        def cast_plane(t):
+            nc.scalar.copy(planes_bf[:, t, :], planes[t][:])
+
+        def gather_scalar(s, t):
+            nc.scalar.activation(x_grouped[s][:, :, t], planes_bf[:, t, :].indirect(slice_offsets(s)), COPY)
+
+        def group_tokens(s):
+            nc.scalar.copy(x_grouped[s][:], gathered[s][:].rearrange("p t n -> p n t"))
+
+        def group_weights(s):
             for i in range(EXPERTS_A_SLICE):
-                nc.scalar.copy(w_grouped[:, i, :, :], w_raw[s * EXPERTS_A_SLICE + i][:].rearrange("p j n -> p n j"))
+                nc.vector.tensor_copy(
+                    w_grouped[s][:, i, :, :], w_raw[s * EXPERTS_A_SLICE + i][:].rearrange("p j n -> p n j")
+                )
+
+        def quantize_weights(s):
             cols = slice(s * SLICE, (s + 1) * SLICE)
             nc.vector.quantize_mx(
                 out=w_codes[:, cols].bitcast(FP8X4),
                 scales=w_scales[:, cols],
-                in_=w_grouped[:].rearrange("p i n j -> p (i n j)"),
+                in_=w_grouped[s][:].rearrange("p i n j -> p (i n j)"),
             )
 
         def quantize_tokens(s):
@@ -95,23 +110,21 @@ def tile_routed_moe_kernel(tc, xT, w, gate, offs, out):
                 in_=x_grouped[s][:].rearrange("p n t -> p (n t)"),
             )
 
-        def multiply(s):
-            for b in range(BLOCKS):
-                acc = psum.tile([P, SLICE], F32, name="acc%d_%d" % (b, s))
-                for i in range(EXPERTS_A_SLICE):
-                    e = s * EXPERTS_A_SLICE + i
-                    feats = slice(e * N + b * P, e * N + (b + 1) * P)
-                    slots = slice(e * C, (e + 1) * C)
-                    nc.tensor.matmul_mx(
-                        out=acc[:, i * C : (i + 1) * C],
-                        lhsT=w_codes[:, feats].bitcast(FP8X4),
-                        lhsT_scale=w_scales[:, feats],
-                        rhs=x_codes[:, slots].bitcast(FP8X4),
-                        rhs_scale=x_scales[:, slots],
-                        start=True,
-                        stop=True,
-                    )
-                nc.scalar.copy(sums[b][s][:], acc[:])
+        def multiply(b, s):
+            for i in range(EXPERTS_A_SLICE):
+                e = s * EXPERTS_A_SLICE + i
+                feats = slice(e * N + b * P, e * N + (b + 1) * P)
+                slots = slice(e * C, (e + 1) * C)
+                nc.tensor.matmul_mx(
+                    out=accs[b][s][:, i * C : (i + 1) * C],
+                    lhsT=w_codes[:, feats].bitcast(FP8X4),
+                    lhsT_scale=w_scales[:, feats],
+                    rhs=x_codes[:, slots].bitcast(FP8X4),
+                    rhs_scale=x_scales[:, slots],
+                    start=True,
+                    stop=True,
+                )
+            nc.scalar.copy(sums[b][s][:], accs[b][s][:])
 
         def scatter(b, s):
             nc.vector.tensor_tensor(
@@ -121,22 +134,35 @@ def tile_routed_moe_kernel(tc, xT, w, gate, offs, out):
                 MULT,
             )
 
-        for s in range(N_SLICES):
-            gather(s, 0)
-        weights(0)
-        for s in range(N_SLICES):
-            gather(s, 1)
-        weights(1)
-        for s in range(N_SLICES):
-            gather(s, 2)
-        weights(2)
-        weights(3)
-        for s in range(N_SLICES):
-            gather(s, 3)
+        for t in range(PACK):
+            gather_vector(0, t)
+            gather_vector(1, t)
+            cast_plane(t)
+        group_tokens(0)
+        group_tokens(1)
+        for s in range(2):
+            group_weights(s)
+            quantize_weights(s)
             quantize_tokens(s)
-            multiply(s)
-        for s in range(N_SLICES):
-            for b in range(BLOCKS):
-                scatter(b, s)
+            multiply(0, s)
+            multiply(1, s)
+        for s in range(2):
+            scatter(0, s)
+            scatter(1, s)
+        for t in range(PACK):
+            gather_scalar(2, t)
+            gather_scalar(3, t)
+        group_weights(2)
+        quantize_weights(2)
+        group_weights(3)
+        quantize_tokens(2)
+        quantize_tokens(3)
+        quantize_weights(3)
+        for s in range(2, N_SLICES):
+            multiply(0, s)
+            multiply(1, s)
+        for s in range(2, N_SLICES):
+            scatter(0, s)
+            scatter(1, s)
         for b in range(BLOCKS):
             nc.sync.dma_start(out[b * P : (b + 1) * P, :], windows[b][:])

@@ -86,12 +86,16 @@ def tile_routed_moe_kernel(tc, xT, w, gate, offs, out):
             nc.scalar.activation(x_grouped[s][:, :, t], planes_bf[:, t, :].indirect(slice_offsets(s)), COPY)
 
         def group_tokens(s):
-            nc.scalar.copy(x_grouped[s][:], gathered[s][:].rearrange("p t n -> p n t"))
+            nc.scalar.copy(
+                x_grouped[s][:].rearrange("p (c q) t -> p c t q", q=4),
+                gathered[s][:].rearrange("p t (c q) -> p c t q", q=4),
+            )
 
         def group_weights(s):
             for i in range(EXPERTS_A_SLICE):
                 nc.vector.tensor_copy(
-                    w_grouped[s][:, i, :, :], w_raw[s * EXPERTS_A_SLICE + i][:].rearrange("p j n -> p n j")
+                    w_grouped[s][:, i, :, :].rearrange("p (c q) j -> p c j q", q=4),
+                    w_raw[s * EXPERTS_A_SLICE + i][:].rearrange("p j (c q) -> p c j q", q=4),
                 )
 
         def quantize_weights(s):

@@ -12,14 +12,14 @@ U16 = mybir.dt.uint16
 U8 = mybir.dt.uint8
 FP8X4 = mybir.dt.float8_e4m3fn_x4
 MULT = mybir.AluOpType.mult
+COPY = mybir.ActivationFunctionType.Copy
 
 P = 128
 PACK = 4
-SLICE = 512
-N_SLICES = E * C // SLICE
-EXPERTS_A_SLICE = SLICE // C
 BLOCKS = N // P
-COPY = mybir.ActivationFunctionType.Copy
+PAIR = 2
+HEAD = 3
+BANKS_A_BLOCK = 4
 
 
 def tile_routed_moe_kernel(tc, xT, w, gate, offs, out):
@@ -32,141 +32,163 @@ def tile_routed_moe_kernel(tc, xT, w, gate, offs, out):
         offsets = lists.tile([P, E * C // 16], U16, name="offsets")
         nc.sync.dma_start(offsets[:], offs)
 
-        def slice_offsets(s):
-            return offsets[:, s * (SLICE // 16) : (s + 1) * (SLICE // 16)]
+        def expert_offsets(e):
+            return offsets[:, e * (C // 16) : (e + 1) * (C // 16)]
+
+        def on(tag, shape, dtype, name):
+            return keep.tile(shape, dtype, name=name, tag=tag, align_bytes=64)
 
         x_rows = xT.rearrange("(p t) n -> p t n", t=PACK)
         planes = [keep.tile([P, T], F32, name="plane%d" % t) for t in range(PACK)]
         planes_bf = keep.tile([P, PACK, T], BF16, name="planes_bf")
         w_raw = [keep.tile([P, PACK, N], F32, name="w_raw%d" % e) for e in range(E)]
-        gates = [keep.tile([P, E * C], F32, name="gate%d" % b) for b in range(BLOCKS)]
-
-        for t in range(PACK):
-            nc.sync.dma_start(planes[t][:], x_rows[:, t, :])
+        gates = {
+            (b, j): keep.tile([P, PAIR * C], F32, name="gate%d_%d" % (b, j))
+            for b in range(BLOCKS)
+            for j in range(E // PAIR)
+        }
 
         def load_w(e):
             nc.sync.dma_start(w_raw[e][:], w[e].rearrange("(p j) n -> p j n", j=PACK))
 
-        for e in range(4):
-            load_w(e)
-        for b in range(BLOCKS):
-            nc.sync.dma_start(gates[b][:], gate[b * P : (b + 1) * P, :])
-        for e in range(4, E):
-            load_w(e)
-
-        w_codes = keep.tile([P, E * N], U32, name="w_codes", align_bytes=64)
-        w_scales = keep.tile([P, E * N], U8, name="w_scales", align_bytes=64)
-        x_codes = keep.tile([P, E * C], U32, name="x_codes", align_bytes=64)
-        x_scales = keep.tile([P, E * C], U8, name="x_scales", align_bytes=64)
-        windows = [keep.tile([P, T], F32, name="window%d" % b) for b in range(BLOCKS)]
-        sums = [
-            [keep.tile([P, SLICE], F32, name="sums%d_%d" % (b, s)) for s in range(N_SLICES)]
-            for b in range(BLOCKS)
-        ]
-        accs = [
-            [psum.tile([P, SLICE], F32, name="acc%d_%d" % (b, s)) for s in range(N_SLICES)]
-            for b in range(BLOCKS)
-        ]
-        gathered = [keep.tile([P, PACK, SLICE], F32, name="gathered%d" % s) for s in range(2)]
-        x_grouped = [
-            keep.tile([P, SLICE, PACK], BF16, name="x_grouped%d" % s, align_bytes=64) for s in range(N_SLICES)
-        ]
-        w_grouped = [
-            keep.tile([P, EXPERTS_A_SLICE, N, PACK], BF16, name="w_grouped%d" % s, align_bytes=64)
-            for s in range(N_SLICES)
-        ]
-
-        def gather_vector(s, t):
-            nc.vector.tensor_copy(gathered[s][:, t, :], planes[t][:].indirect(slice_offsets(s)))
-
-        def cast_plane(t):
-            nc.scalar.copy(planes_bf[:, t, :], planes[t][:])
-
-        def gather_scalar(s, t):
-            nc.scalar.activation(x_grouped[s][:, :, t], planes_bf[:, t, :].indirect(slice_offsets(s)), COPY)
-
-        def group_tokens(s):
-            nc.scalar.copy(
-                x_grouped[s][:].rearrange("p (c q) t -> p c t q", q=4),
-                gathered[s][:].rearrange("p t (c q) -> p c t q", q=4),
-            )
-
-        def group_weights(s):
-            for i in range(EXPERTS_A_SLICE):
-                nc.vector.tensor_copy(
-                    w_grouped[s][:, i, :, :].rearrange("p (c q) j -> p c j q", q=4),
-                    w_raw[s * EXPERTS_A_SLICE + i][:].rearrange("p j (c q) -> p c j q", q=4),
+        def load_gate(j):
+            for b in range(BLOCKS):
+                nc.sync.dma_start(
+                    gates[b, j][:], gate[b * P : (b + 1) * P, j * PAIR * C : (j + 1) * PAIR * C]
                 )
 
-        def quantize_weights(s):
-            cols = slice(s * SLICE, (s + 1) * SLICE)
+        for t in range(PACK):
+            nc.sync.dma_start(planes[t][:], x_rows[:, t, :])
+        for e in range(4):
+            load_w(e)
+        load_gate(0)
+        for e in range(4, E):
+            load_w(e)
+        for j in range(1, E // PAIR):
+            load_gate(j)
+
+        windows = [keep.tile([P, T], F32, name="window%d" % b) for b in range(BLOCKS)]
+        w_scales = [keep.tile([P, PAIR * N], U8, name="w_scales%d" % j, align_bytes=64) for j in range(E // PAIR)]
+        w_grouped = {}
+        w_codes = {}
+        x_grouped = {}
+        x_codes = {}
+        x_scales = {}
+        sums = {}
+
+        def cast_plane(t):
+            nc.vector.tensor_copy(planes_bf[:, t, :], planes[t][:])
+
+        def gather(e, t):
+            nc.scalar.activation(x_grouped[e][:, :, t], planes_bf[:, t, :].indirect(expert_offsets(e)), COPY)
+
+        def gather_expert(e, tag):
+            x_grouped[e] = on(tag, [P, C, PACK], BF16, "x_grouped%d" % e)
+            for t in range(PACK):
+                gather(e, t)
+
+        def group_weights(j, tag, copy):
+            w_grouped[j] = on(tag, [P, PAIR, N, PACK], BF16, "w_grouped%d" % j)
+            for i in range(PAIR):
+                copy(
+                    w_grouped[j][:, i, :, :].rearrange("p (c q) j -> p c j q", q=4),
+                    w_raw[j * PAIR + i][:].rearrange("p j (c q) -> p c j q", q=4),
+                )
+
+        def quantize_weights(j, tag):
+            w_codes[j] = on(tag, [P, PAIR * N], U32, "w_codes%d" % j)
             nc.vector.quantize_mx(
-                out=w_codes[:, cols].bitcast(FP8X4),
-                scales=w_scales[:, cols],
-                in_=w_grouped[s][:].rearrange("p i n j -> p (i n j)"),
+                out=w_codes[j][:].bitcast(FP8X4),
+                scales=w_scales[j][:],
+                in_=w_grouped[j][:].rearrange("p i n j -> p (i n j)"),
             )
 
-        def quantize_tokens(s):
-            cols = slice(s * SLICE, (s + 1) * SLICE)
+        def quantize_tokens(e, tag):
+            x_codes[e] = on(tag, [P, C], U32, "x_codes%d" % e)
+            x_scales[e] = on("x_scales%d" % e, [P, C], U8, "x_scales%d" % e)
             nc.vector.quantize_mx(
-                out=x_codes[:, cols].bitcast(FP8X4),
-                scales=x_scales[:, cols],
-                in_=x_grouped[s][:].rearrange("p n t -> p (n t)"),
+                out=x_codes[e][:].bitcast(FP8X4),
+                scales=x_scales[e][:],
+                in_=x_grouped[e][:].rearrange("p n t -> p (n t)"),
             )
 
-        def multiply(b, s):
-            for i in range(EXPERTS_A_SLICE):
-                e = s * EXPERTS_A_SLICE + i
-                feats = slice(e * N + b * P, e * N + (b + 1) * P)
-                slots = slice(e * C, (e + 1) * C)
+        def multiply(e):
+            accs = []
+            for b in range(BLOCKS):
+                acc = psum.tile([P, C], F32, name="acc%d_%d" % (b, e), tag="acc%d_%d" % (b, e % BANKS_A_BLOCK))
+                feats = slice((e % PAIR) * N + b * P, (e % PAIR) * N + (b + 1) * P)
                 nc.tensor.matmul_mx(
-                    out=accs[b][s][:, i * C : (i + 1) * C],
-                    lhsT=w_codes[:, feats].bitcast(FP8X4),
-                    lhsT_scale=w_scales[:, feats],
-                    rhs=x_codes[:, slots].bitcast(FP8X4),
-                    rhs_scale=x_scales[:, slots],
+                    out=acc[:],
+                    lhsT=w_codes[e // PAIR][:, feats].bitcast(FP8X4),
+                    lhsT_scale=w_scales[e // PAIR][:, feats],
+                    rhs=x_codes[e][:].bitcast(FP8X4),
+                    rhs_scale=x_scales[e][:],
                     start=True,
                     stop=True,
                 )
-            nc.scalar.copy(sums[b][s][:], accs[b][s][:])
+                accs.append(acc)
+            for b in range(BLOCKS):
+                sums[b, e] = on("sums%d_%d" % (b, e), [P, C], F32, "sums%d_%d" % (b, e))
+                nc.scalar.copy(sums[b, e][:], accs[b][:])
 
-        def scatter(b, s):
+        def scatter(b, e):
             nc.vector.tensor_tensor(
-                windows[b][:].indirect(slice_offsets(s)),
-                sums[b][s][:],
-                gates[b][:, s * SLICE : (s + 1) * SLICE],
+                windows[b][:].indirect(expert_offsets(e)),
+                sums[b, e][:],
+                gates[b, e // PAIR][:, (e % PAIR) * C : (e % PAIR + 1) * C],
                 MULT,
             )
 
+        for e in range(HEAD):
+            x_grouped[e] = on("x_grouped%d" % e, [P, C, PACK], BF16, "x_grouped%d" % e)
         for t in range(PACK):
-            gather_vector(0, t)
-            gather_vector(1, t)
             cast_plane(t)
-        group_tokens(0)
-        group_tokens(1)
-        for s in range(2):
-            group_weights(s)
-            quantize_weights(s)
-            quantize_tokens(s)
-            multiply(0, s)
-            multiply(1, s)
-        for s in range(2):
-            scatter(0, s)
-            scatter(1, s)
-        for t in range(PACK):
-            gather_scalar(2, t)
-            gather_scalar(3, t)
-        group_weights(2)
-        quantize_weights(2)
-        group_weights(3)
-        quantize_tokens(2)
-        quantize_tokens(3)
-        quantize_weights(3)
-        for s in range(2, N_SLICES):
-            multiply(0, s)
-            multiply(1, s)
-        for s in range(2, N_SLICES):
-            scatter(0, s)
-            scatter(1, s)
+            for e in range(HEAD):
+                gather(e, t)
+        group_weights(0, "w_grouped0", nc.vector.tensor_copy)
+        quantize_weights(0, "w_codes0")
+        quantize_tokens(0, "w_grouped0")
+        multiply(0)
+        quantize_tokens(1, "x_grouped0")
+        multiply(1)
+        group_weights(1, "w_grouped1", nc.vector.tensor_copy)
+        quantize_weights(1, "w_codes1")
+        quantize_tokens(2, "x_grouped1")
+        multiply(2)
+        group_weights(2, "x_scales0", nc.scalar.copy)
+        gather_expert(3, "x_scales1")
+        gather_expert(4, "x_scales2")
+        scatter(0, 0)
+        scatter(1, 0)
+        scatter(0, 1)
+        quantize_tokens(3, "sums0_1")
+        multiply(3)
+        group_weights(3, "sums0_1", nc.scalar.copy)
+        gather_expert(5, "x_scales3")
+        scatter(1, 1)
+        quantize_weights(2, "sums1_1")
+        scatter(0, 2)
+        quantize_tokens(4, "sums0_2")
+        multiply(4)
+        gather_expert(6, "x_scales4")
+        scatter(1, 2)
+        scatter(0, 3)
+        quantize_tokens(5, "sums0_3")
+        multiply(5)
+        gather_expert(7, "x_scales5")
+        scatter(1, 3)
+        quantize_weights(3, "sums1_3")
+        scatter(0, 4)
+        quantize_tokens(6, "sums0_4")
+        multiply(6)
+        scatter(1, 4)
+        scatter(0, 5)
+        quantize_tokens(7, "sums0_5")
+        multiply(7)
+        scatter(1, 5)
+        scatter(0, 6)
+        scatter(1, 6)
+        scatter(0, 7)
+        scatter(1, 7)
         for b in range(BLOCKS):
             nc.sync.dma_start(out[b * P : (b + 1) * P, :], windows[b][:])

@@ -18,7 +18,7 @@ P = 128
 PACK = 4
 BLOCKS = N // P
 PAIR = 2
-HEAD = 3
+HEAD = 4
 BANKS_A_BLOCK = 4
 
 
@@ -82,6 +82,9 @@ def tile_routed_moe_kernel(tc, xT, w, gate, offs, out):
         def gather(e, t):
             nc.scalar.activation(x_grouped[e][:, :, t], planes_bf[:, t, :].indirect(expert_offsets(e)), COPY)
 
+        def gather_vector(e, t):
+            nc.vector.tensor_copy(x_grouped[e][:, :, t], planes[t][:].indirect(expert_offsets(e)))
+
         def gather_expert(e, tag):
             x_grouped[e] = on(tag, [P, C, PACK], BF16, "x_grouped%d" % e)
             for t in range(PACK):
@@ -143,28 +146,28 @@ def tile_routed_moe_kernel(tc, xT, w, gate, offs, out):
             x_grouped[e] = on("x_grouped%d" % e, [P, C, PACK], BF16, "x_grouped%d" % e)
         for t in range(PACK):
             cast_plane(t)
-            for e in range(HEAD):
+            gather_vector(0, t)
+            for e in range(1, HEAD):
                 gather(e, t)
         group_weights(0, "w_grouped0", nc.vector.tensor_copy)
         quantize_weights(0, "w_codes0")
         quantize_tokens(0, "w_grouped0")
         multiply(0)
+        group_weights(1, "x_scales0", nc.scalar.copy)
         quantize_tokens(1, "x_grouped0")
         multiply(1)
-        group_weights(1, "w_grouped1", nc.vector.tensor_copy)
+        group_weights(2, "x_scales1", nc.scalar.copy)
         quantize_weights(1, "w_codes1")
         quantize_tokens(2, "x_grouped1")
         multiply(2)
-        group_weights(2, "x_scales0", nc.scalar.copy)
-        gather_expert(3, "x_scales1")
         gather_expert(4, "x_scales2")
+        quantize_tokens(3, "x_grouped2")
+        multiply(3)
+        group_weights(3, "x_grouped2", nc.scalar.copy)
+        gather_expert(5, "x_scales3")
         scatter(0, 0)
         scatter(1, 0)
         scatter(0, 1)
-        quantize_tokens(3, "sums0_1")
-        multiply(3)
-        group_weights(3, "sums0_1", nc.scalar.copy)
-        gather_expert(5, "x_scales3")
         scatter(1, 1)
         quantize_weights(2, "sums1_1")
         scatter(0, 2)
@@ -172,12 +175,12 @@ def tile_routed_moe_kernel(tc, xT, w, gate, offs, out):
         multiply(4)
         gather_expert(6, "x_scales4")
         scatter(1, 2)
+        quantize_weights(3, "sums1_2")
         scatter(0, 3)
         quantize_tokens(5, "sums0_3")
         multiply(5)
         gather_expert(7, "x_scales5")
         scatter(1, 3)
-        quantize_weights(3, "sums1_3")
         scatter(0, 4)
         quantize_tokens(6, "sums0_4")
         multiply(6)

@@ -41,7 +41,7 @@ def tile_routed_moe_kernel(tc, xT, w, gate, offs, out):
         x_rows = xT.rearrange("(p t) n -> p t n", t=PACK)
         planes = [keep.tile([P, T], F32, name="plane%d" % t) for t in range(PACK)]
         planes_bf = keep.tile([P, PACK, T], BF16, name="planes_bf")
-        w_raw = [keep.tile([P, PACK, N], F32, name="w_raw%d" % e) for e in range(E)]
+        w_raw = [on("w_raw%d" % e, [P, PACK, N], F32, "w_raw%d" % e) for e in range(E)]
         gates = {
             (b, j): keep.tile([P, PAIR * C], F32, name="gate%d_%d" % (b, j))
             for b in range(BLOCKS)
@@ -150,11 +150,11 @@ def tile_routed_moe_kernel(tc, xT, w, gate, offs, out):
             for e in range(1, HEAD):
                 gather(e, t)
         group_weights(0, "w_grouped0", nc.vector.tensor_copy)
-        quantize_weights(0, "w_codes0")
-        quantize_tokens(0, "w_grouped0")
+        quantize_tokens(0, "w_raw1")
+        quantize_weights(0, "x_grouped0")
         multiply(0)
         group_weights(1, "x_scales0", nc.scalar.copy)
-        quantize_tokens(1, "x_grouped0")
+        quantize_tokens(1, "w_grouped0")
         multiply(1)
         group_weights(2, "x_scales1", nc.scalar.copy)
         quantize_weights(1, "w_codes1")

from contextlib import ExitStack

import concourse.mybir as mybir

K, T, E, C, N = 512, 2048, 8, 256, 256
FLOPS = 2 * K * N * E * C

F32 = mybir.dt.float32
BF16 = mybir.dt.bfloat16
U32 = mybir.dt.uint32
U16 = mybir.dt.uint16
U8 = mybir.dt.uint8
FP8X4 = mybir.dt.float8_e4m3fn_x4
MULT = mybir.AluOpType.mult
COPY = mybir.ActivationFunctionType.Copy

P = 128
PACK = 4
BLOCKS = N // P
PAIR = 2
HEAD = 4
BANKS_A_BLOCK = 4


def tile_routed_moe_kernel(tc, xT, w, gate, offs, out):
    nc = tc.nc
    with ExitStack() as ctx:
        lists = ctx.enter_context(tc.tile_pool(name="lists", bufs=1))
        keep = ctx.enter_context(tc.tile_pool(name="keep", bufs=1))
        psum = ctx.enter_context(tc.psum_pool(name="psum", bufs=1))

        offsets = lists.tile([P, E * C // 16], U16, name="offsets")
        nc.sync.dma_start(offsets[:], offs)

        def expert_offsets(e):
            return offsets[:, e * (C // 16) : (e + 1) * (C // 16)]

        def on(tag, shape, dtype, name):
            return keep.tile(shape, dtype, name=name, tag=tag, align_bytes=64)

        x_rows = xT.rearrange("(p t) n -> p t n", t=PACK)
        planes = [keep.tile([P, T], F32, name="plane%d" % t) for t in range(PACK)]
        planes_bf = keep.tile([P, PACK, T], BF16, name="planes_bf")
        w_raw = [on("w_raw%d" % e, [P, PACK, N], F32, "w_raw%d" % e) for e in range(E)]
        gates = {
            (b, j): keep.tile([P, PAIR * C], F32, name="gate%d_%d" % (b, j))
            for b in range(BLOCKS)
            for j in range(E // PAIR)
        }

        def load_w(e):
            nc.sync.dma_start(w_raw[e][:], w[e].rearrange("(p j) n -> p j n", j=PACK))

        def load_gate(j):
            for b in range(BLOCKS):
                nc.sync.dma_start(
                    gates[b, j][:], gate[b * P : (b + 1) * P, j * PAIR * C : (j + 1) * PAIR * C]
                )

        for t in range(PACK):
            nc.sync.dma_start(planes[t][:], x_rows[:, t, :])
        for e in range(4):
            load_w(e)
        load_gate(0)
        for e in range(4, E):
            load_w(e)
        for j in range(1, E // PAIR):
            load_gate(j)

        windows = [keep.tile([P, T], F32, name="window%d" % b) for b in range(BLOCKS)]
        w_scales = [keep.tile([P, PAIR * N], U8, name="w_scales%d" % j, align_bytes=64) for j in range(E // PAIR)]
        w_grouped = {}
        w_codes = {}
        x_grouped = {}
        x_codes = {}
        x_scales = {}
        sums = {}

        def cast_plane(t):
            nc.vector.tensor_copy(planes_bf[:, t, :], planes[t][:])

        def gather(e, t):
            nc.scalar.activation(x_grouped[e][:, :, t], planes_bf[:, t, :].indirect(expert_offsets(e)), COPY)

        def gather_vector(e, t):
            nc.vector.tensor_copy(x_grouped[e][:, :, t], planes[t][:].indirect(expert_offsets(e)))

        def gather_expert(e, tag):
            x_grouped[e] = on(tag, [P, C, PACK], BF16, "x_grouped%d" % e)
            for t in range(PACK):
                gather(e, t)

        def group_weights(j, tag, copy):
            w_grouped[j] = on(tag, [P, PAIR, N, PACK], BF16, "w_grouped%d" % j)
            for i in range(PAIR):
                copy(
                    w_grouped[j][:, i, :, :].rearrange("p (c q) j -> p c j q", q=4),
                    w_raw[j * PAIR + i][:].rearrange("p j (c q) -> p c j q", q=4),
                )

        def quantize_weights(j, tag):
            w_codes[j] = on(tag, [P, PAIR * N], U32, "w_codes%d" % j)
            nc.vector.quantize_mx(
                out=w_codes[j][:].bitcast(FP8X4),
                scales=w_scales[j][:],
                in_=w_grouped[j][:].rearrange("p i n j -> p (i n j)"),
            )

        def quantize_tokens(e, tag):
            x_codes[e] = on(tag, [P, C], U32, "x_codes%d" % e)
            x_scales[e] = on("x_scales%d" % e, [P, C], U8, "x_scales%d" % e)
            nc.vector.quantize_mx(
                out=x_codes[e][:].bitcast(FP8X4),
                scales=x_scales[e][:],
                in_=x_grouped[e][:].rearrange("p n t -> p (n t)"),
            )

        def multiply(e):
            accs = []
            for b in range(BLOCKS):
                acc = psum.tile([P, C], F32, name="acc%d_%d" % (b, e), tag="acc%d_%d" % (b, e % BANKS_A_BLOCK))
                feats = slice((e % PAIR) * N + b * P, (e % PAIR) * N + (b + 1) * P)
                nc.tensor.matmul_mx(
                    out=acc[:],
                    lhsT=w_codes[e // PAIR][:, feats].bitcast(FP8X4),
                    lhsT_scale=w_scales[e // PAIR][:, feats],
                    rhs=x_codes[e][:].bitcast(FP8X4),
                    rhs_scale=x_scales[e][:],
                    start=True,
                    stop=True,
                )
                accs.append(acc)
            for b in range(BLOCKS):
                sums[b, e] = on("sums%d_%d" % (b, e), [P, C], F32, "sums%d_%d" % (b, e))
                nc.scalar.copy(sums[b, e][:], accs[b][:])

        def scatter(b, e):
            nc.vector.tensor_tensor(
                windows[b][:].indirect(expert_offsets(e)),
                sums[b, e][:],
                gates[b, e // PAIR][:, (e % PAIR) * C : (e % PAIR + 1) * C],
                MULT,
            )

        for e in range(HEAD):
            x_grouped[e] = on("x_grouped%d" % e, [P, C, PACK], BF16, "x_grouped%d" % e)
        for t in range(PACK):
            cast_plane(t)
            gather_vector(0, t)
            for e in range(1, HEAD):
                gather(e, t)
        group_weights(0, "w_grouped0", nc.vector.tensor_copy)
        quantize_tokens(0, "w_raw1")
        quantize_weights(0, "x_grouped0")
        multiply(0)
        group_weights(1, "x_scales0", nc.scalar.copy)
        quantize_tokens(1, "w_grouped0")
        multiply(1)
        group_weights(2, "x_scales1", nc.scalar.copy)
        quantize_weights(1, "w_codes1")
        quantize_tokens(2, "x_grouped1")
        multiply(2)
        gather_expert(4, "x_scales2")
        quantize_tokens(3, "x_grouped2")
        multiply(3)
        group_weights(3, "x_grouped2", nc.scalar.copy)
        gather_expert(5, "x_scales3")
        scatter(0, 0)
        scatter(1, 0)
        scatter(0, 1)
        scatter(1, 1)
        quantize_weights(2, "sums1_1")
        scatter(0, 2)
        quantize_tokens(4, "sums0_2")
        multiply(4)
        gather_expert(6, "x_scales4")
        scatter(1, 2)
        quantize_weights(3, "sums1_2")
        scatter(0, 3)
        quantize_tokens(5, "sums0_3")
        multiply(5)
        gather_expert(7, "x_scales5")
        scatter(1, 3)
        scatter(0, 4)
        quantize_tokens(6, "sums0_4")
        multiply(6)
        scatter(1, 4)
        scatter(0, 5)
        quantize_tokens(7, "sums0_5")
        multiply(7)
        scatter(1, 5)
        scatter(0, 6)
        scatter(1, 6)
        scatter(0, 7)
        scatter(1, 7)
        for b in range(BLOCKS):
            nc.sync.dma_start(out[b * P : (b + 1) * P, :], windows[b][:])
